import numpy as np
import ml_dtypes

BF16 = ml_dtypes.bfloat16


def bf(x):
    return np.asarray(x, np.float32).astype(BF16)


def f32(x):
    return np.asarray(x, np.float32)


def f64(x):
    return np.asarray(x).astype(np.float64)


def striped(idx):
    return np.tile(idx.reshape(-1, 16).T, (8, 1))


S, K, M, N = 2048, 256, 128, 2048


def setup_inputs():
    return {"table": bf(np.random.standard_normal((K, S))), "w": bf(np.random.standard_normal((K, M)) / np.sqrt(K)), "b": f32(0.5 * np.random.standard_normal((M, 1))), "offs": striped(np.random.permutation(np.tile(np.arange(S), 2))[:N])}


def reference(table, w, b, offs):
    idx = offs[:16].T.reshape(-1)
    x = f64(table)[:, idx]
    y = f64(w).T @ x
    return y + f64(b)

@@ -1,0 +1,56 @@
+import concourse.mybir as mybir
+
+BF16, F32, U16 = mybir.dt.bfloat16, mybir.dt.float32, mybir.dt.uint16
+
+P = 128
+S = 2048
+K = 256
+M = 128
+N = 2048
+K_BLOCKS = K // P
+PIECE = 512
+PIECES = N // PIECE
+PIECE_COLS = PIECE // 16
+
+FLOPS = 2 * K * M * N
+
+
+def tile_gather_matmul_kernel(tc, table, w, b, offs, out):
+    nc = tc.nc
+    with (
+        tc.tile_pool(name="held", bufs=1) as held,
+        tc.psum_pool(name="psum", bufs=1) as psum,
+    ):
+        offsets = held.tile([P, N // 16], U16, name="offsets")
+        nc.sync.dma_start(offsets[:], offs)
+        windows = []
+        for k in range(K_BLOCKS):
+            window = held.tile([P, S], BF16, name=f"window{k}")
+            nc.sync.dma_start(window[:], table[k * P : (k + 1) * P, :])
+            windows.append(window)
+        weights = held.tile([P, K_BLOCKS, M], BF16, name="weights")
+        nc.scalar.dma_start(weights[:], w.rearrange("(k p) m -> p k m", p=P))
+        bias = held.tile([P, 1], F32, name="bias")
+        nc.scalar.dma_start(bias[:], b)
+
+        banks = [psum.tile([P, PIECE], F32, name=f"bank{i}") for i in range(PIECES)]
+        for k in range(K_BLOCKS):
+            for i in range(PIECES):
+                nc.tensor.matmul(
+                    banks[i][:],
+                    weights[:, k, :],
+                    windows[k][:].indirect(offsets[:, i * PIECE_COLS : (i + 1) * PIECE_COLS]),
+                    start=(k == 0),
+                    stop=(k == K_BLOCKS - 1),
+                )
+
+        for i in range(PIECES):
+            staged = held.tile([P, PIECE], F32, name=f"staged{i}")
+            if i % 2 == 0:
+                nc.vector.tensor_scalar_add(staged[:], banks[i][:], bias[:, 0:1])
+                nc.sync.dma_start(out[:, i * PIECE : (i + 1) * PIECE], staged[:])
+            else:
+                nc.scalar.activation(
+                    staged[:], banks[i][:], mybir.ActivationFunctionType.Identity, bias=bias[:, 0:1]
+                )
+                nc.scalar.dma_start(out[:, i * PIECE : (i + 1) * PIECE], staged[:])

@@ -8,15 +8,17 @@ K = 256
 M = 128
 N = 2048
 K_BLOCKS = K // P
-PIECE = 512
-PIECES = N // PIECE
-PIECE_COLS = PIECE // 16
+BANK = 512
+WIDTHS = (BANK, BANK, BANK, BANK // 2, BANK // 2)
+assert sum(WIDTHS) == N
+WARM_UPS = 6
 
 FLOPS = 2 * K * M * N
 
 
 def tile_gather_matmul_kernel(tc, table, w, b, offs, out):
     nc = tc.nc
+    firsts = [sum(WIDTHS[:i]) for i in range(len(WIDTHS))]
     with (
         tc.tile_pool(name="held", bufs=1) as held,
         tc.psum_pool(name="psum", bufs=1) as psum,
@@ -33,24 +35,37 @@ def tile_gather_matmul_kernel(tc, table, w, b, offs, out):
         bias = held.tile([P, 1], F32, name="bias")
         nc.scalar.dma_start(bias[:], b)
 
-        banks = [psum.tile([P, PIECE], F32, name=f"bank{i}") for i in range(PIECES)]
+        zeros = held.tile([P, M], BF16, name="zeros")
+        nc.vector.memset(zeros[:], 0.0)
+        unread = psum.tile([P, BANK // M, M], F32, name="unread")
+        for turn in range(WARM_UPS):
+            nc.tensor.matmul(
+                unread[:],
+                zeros[:],
+                zeros[:].unsqueeze(1).to_broadcast([P, BANK // M, M]),
+                start=True,
+                stop=True,
+            )
+
+        banks = [psum.tile([P, width], F32, name=f"bank{i}") for i, width in enumerate(WIDTHS)]
         for k in range(K_BLOCKS):
-            for i in range(PIECES):
+            for bank, first, width in zip(banks, firsts, WIDTHS):
+                piece = offsets[:, first // 16 : (first + width) // 16]
                 nc.tensor.matmul(
-                    banks[i][:],
+                    bank[:],
                     weights[:, k, :],
-                    windows[k][:].indirect(offsets[:, i * PIECE_COLS : (i + 1) * PIECE_COLS]),
+                    windows[k][:].indirect(piece),
                     start=(k == 0),
                     stop=(k == K_BLOCKS - 1),
                 )
 
-        for i in range(PIECES):
-            staged = held.tile([P, PIECE], F32, name=f"staged{i}")
+        for i, (bank, first, width) in enumerate(zip(banks, firsts, WIDTHS)):
+            staged = held.tile([P, width], F32, name=f"staged{i}")
             if i % 2 == 0:
-                nc.vector.tensor_scalar_add(staged[:], banks[i][:], bias[:, 0:1])
-                nc.sync.dma_start(out[:, i * PIECE : (i + 1) * PIECE], staged[:])
+                nc.vector.tensor_scalar_add(staged[:], bank[:], bias[:, 0:1])
+                nc.sync.dma_start(out[:, first : first + width], staged[:])
             else:
                 nc.scalar.activation(
-                    staged[:], banks[i][:], mybir.ActivationFunctionType.Identity, bias=bias[:, 0:1]
+                    staged[:], bank[:], mybir.ActivationFunctionType.Identity, bias=bias[:, 0:1]
                 )
-                nc.scalar.dma_start(out[:, i * PIECE : (i + 1) * PIECE], staged[:])
+                nc.scalar.dma_start(out[:, first : first + width], staged[:])

@@ -11,17 +11,15 @@ K_BLOCKS = K // P
 BANK = 512
 WIDTHS = (BANK, BANK, BANK, BANK // 2, BANK // 2)
 assert sum(WIDTHS) == N
-WARM_UPS = 6
 
 FLOPS = 2 * K * M * N
 
 
 def tile_gather_matmul_kernel(tc, table, w, b, offs, out):
     nc = tc.nc
-    firsts = [sum(WIDTHS[:i]) for i in range(len(WIDTHS))]
     with (
         tc.tile_pool(name="held", bufs=1) as held,
-        tc.psum_pool(name="psum", bufs=1) as psum,
+        tc.psum_pool(name="psum", bufs=4) as psum,
     ):
         offsets = held.tile([P, N // 16], U16, name="offsets")
         nc.sync.dma_start(offsets[:], offs)
@@ -35,37 +33,28 @@ def tile_gather_matmul_kernel(tc, table, w, b, offs, out):
         bias = held.tile([P, 1], F32, name="bias")
         nc.scalar.dma_start(bias[:], b)
 
-        zeros = held.tile([P, M], BF16, name="zeros")
-        nc.vector.memset(zeros[:], 0.0)
-        unread = psum.tile([P, BANK // M, M], F32, name="unread")
-        for turn in range(WARM_UPS):
-            nc.tensor.matmul(
-                unread[:],
-                zeros[:],
-                zeros[:].unsqueeze(1).to_broadcast([P, BANK // M, M]),
-                start=True,
-                stop=True,
-            )
-
-        banks = [psum.tile([P, width], F32, name=f"bank{i}") for i, width in enumerate(WIDTHS)]
-        for k in range(K_BLOCKS):
-            for bank, first, width in zip(banks, firsts, WIDTHS):
-                piece = offsets[:, first // 16 : (first + width) // 16]
+        staged = held.tile([P, N], F32, name="staged")
+        first = 0
+        for i, width in enumerate(WIDTHS):
+            columns = slice(first, first + width)
+            bank = psum.tile([P, width], F32, name="bank")
+            for k in range(K_BLOCKS):
                 nc.tensor.matmul(
                     bank[:],
                     weights[:, k, :],
-                    windows[k][:].indirect(piece),
+                    windows[k][:].indirect(offsets[:, first // 16 : (first + width) // 16]),
                     start=(k == 0),
                     stop=(k == K_BLOCKS - 1),
                 )
-
-        for i, (bank, first, width) in enumerate(zip(banks, firsts, WIDTHS)):
-            staged = held.tile([P, width], F32, name=f"staged{i}")
             if i % 2 == 0:
-                nc.vector.tensor_scalar_add(staged[:], bank[:], bias[:, 0:1])
-                nc.sync.dma_start(out[:, first : first + width], staged[:])
+                nc.vector.tensor_scalar_add(staged[:, columns], bank[:], bias[:, 0:1])
+                nc.sync.dma_start(out[:, columns], staged[:, columns])
             else:
                 nc.scalar.activation(
-                    staged[:], bank[:], mybir.ActivationFunctionType.Identity, bias=bias[:, 0:1]
+                    staged[:, columns],
+                    bank[:],
+                    mybir.ActivationFunctionType.Identity,
+                    bias=bias[:, 0:1],
                 )
-                nc.scalar.dma_start(out[:, first : first + width], staged[:])
+                nc.scalar.dma_start(out[:, columns], staged[:, columns])
+            first += width

@@ -11,6 +11,7 @@ K_BLOCKS = K // P
 BANK = 512
 WIDTHS = (BANK, BANK, BANK, BANK // 2, BANK // 2)
 assert sum(WIDTHS) == N
+WARM_UPS = 4
 
 FLOPS = 2 * K * M * N
 
@@ -19,6 +20,7 @@ def tile_gather_matmul_kernel(tc, table, w, b, offs, out):
     nc = tc.nc
     with (
         tc.tile_pool(name="held", bufs=1) as held,
+        tc.psum_pool(name="spare", bufs=1) as spare,
         tc.psum_pool(name="psum", bufs=4) as psum,
     ):
         offsets = held.tile([P, N // 16], U16, name="offsets")
@@ -32,6 +34,18 @@ def tile_gather_matmul_kernel(tc, table, w, b, offs, out):
         nc.scalar.dma_start(weights[:], w.rearrange("(k p) m -> p k m", p=P))
         bias = held.tile([P, 1], F32, name="bias")
         nc.scalar.dma_start(bias[:], b)
+
+        zeros = held.tile([P, M], BF16, name="zeros")
+        nc.vector.memset(zeros[:], 0.0)
+        unread = spare.tile([P, BANK // M, M], F32, name="unread")
+        for turn in range(WARM_UPS):
+            nc.tensor.matmul(
+                unread[:],
+                zeros[:],
+                zeros[:].unsqueeze(1).to_broadcast([P, BANK // M, M]),
+                start=True,
+                stop=True,
+            )
 
         staged = held.tile([P, N], F32, name="staged")
         first = 0

@@ -12,6 +12,7 @@ BANK = 512
 WIDTHS = (BANK, BANK, BANK, BANK // 2, BANK // 2)
 assert sum(WIDTHS) == N
 WARM_UPS = 4
+EARLY_PIECES = 3
 
 FLOPS = 2 * K * M * N
 
@@ -21,7 +22,7 @@ def tile_gather_matmul_kernel(tc, table, w, b, offs, out):
     with (
         tc.tile_pool(name="held", bufs=1) as held,
         tc.psum_pool(name="spare", bufs=1) as spare,
-        tc.psum_pool(name="psum", bufs=4) as psum,
+        tc.psum_pool(name="psum", bufs=len(WIDTHS)) as psum,
     ):
         offsets = held.tile([P, N // 16], U16, name="offsets")
         nc.sync.dma_start(offsets[:], offs)
@@ -52,13 +53,14 @@ def tile_gather_matmul_kernel(tc, table, w, b, offs, out):
         for i, width in enumerate(WIDTHS):
             columns = slice(first, first + width)
             bank = psum.tile([P, width], F32, name="bank")
-            for k in range(K_BLOCKS):
+            blocks = (0, 1) if i < EARLY_PIECES else (1, 0)
+            for turn, k in enumerate(blocks):
                 nc.tensor.matmul(
                     bank[:],
                     weights[:, k, :],
                     windows[k][:].indirect(offsets[:, first // 16 : (first + width) // 16]),
-                    start=(k == 0),
-                    stop=(k == K_BLOCKS - 1),
+                    start=(turn == 0),
+                    stop=(turn == K_BLOCKS - 1),
                 )
             if i % 2 == 0:
                 nc.vector.tensor_scalar_add(staged[:, columns], bank[:], bias[:, 0:1])

@@ -11,7 +11,6 @@ K_BLOCKS = K // P
 BANK = 512
 WIDTHS = (BANK, BANK, BANK, BANK // 2, BANK // 2)
 assert sum(WIDTHS) == N
-WARM_UPS = 4
 EARLY_PIECES = 3
 
 FLOPS = 2 * K * M * N
@@ -21,7 +20,6 @@ def tile_gather_matmul_kernel(tc, table, w, b, offs, out):
     nc = tc.nc
     with (
         tc.tile_pool(name="held", bufs=1) as held,
-        tc.psum_pool(name="spare", bufs=1) as spare,
         tc.psum_pool(name="psum", bufs=len(WIDTHS)) as psum,
     ):
         offsets = held.tile([P, N // 16], U16, name="offsets")
@@ -35,18 +33,6 @@ def tile_gather_matmul_kernel(tc, table, w, b, offs, out):
         nc.scalar.dma_start(weights[:], w.rearrange("(k p) m -> p k m", p=P))
         bias = held.tile([P, 1], F32, name="bias")
         nc.scalar.dma_start(bias[:], b)
-
-        zeros = held.tile([P, M], BF16, name="zeros")
-        nc.vector.memset(zeros[:], 0.0)
-        unread = spare.tile([P, BANK // M, M], F32, name="unread")
-        for turn in range(WARM_UPS):
-            nc.tensor.matmul(
-                unread[:],
-                zeros[:],
-                zeros[:].unsqueeze(1).to_broadcast([P, BANK // M, M]),
-                start=True,
-                stop=True,
-            )
 
         staged = held.tile([P, N], F32, name="staged")
         first = 0

import concourse.mybir as mybir

BF16, F32, U16 = mybir.dt.bfloat16, mybir.dt.float32, mybir.dt.uint16

P = 128
S = 2048
K = 256
M = 128
N = 2048
K_BLOCKS = K // P
BANK = 512
WIDTHS = (BANK, BANK, BANK, BANK // 2, BANK // 2)
assert sum(WIDTHS) == N
EARLY_PIECES = 3

FLOPS = 2 * K * M * N


def tile_gather_matmul_kernel(tc, table, w, b, offs, out):
    nc = tc.nc
    with (
        tc.tile_pool(name="held", bufs=1) as held,
        tc.psum_pool(name="psum", bufs=len(WIDTHS)) as psum,
    ):
        offsets = held.tile([P, N // 16], U16, name="offsets")
        nc.sync.dma_start(offsets[:], offs)
        windows = []
        for k in range(K_BLOCKS):
            window = held.tile([P, S], BF16, name=f"window{k}")
            nc.sync.dma_start(window[:], table[k * P : (k + 1) * P, :])
            windows.append(window)
        weights = held.tile([P, K_BLOCKS, M], BF16, name="weights")
        nc.scalar.dma_start(weights[:], w.rearrange("(k p) m -> p k m", p=P))
        bias = held.tile([P, 1], F32, name="bias")
        nc.scalar.dma_start(bias[:], b)

        staged = held.tile([P, N], F32, name="staged")
        first = 0
        for i, width in enumerate(WIDTHS):
            columns = slice(first, first + width)
            bank = psum.tile([P, width], F32, name="bank")
            blocks = (0, 1) if i < EARLY_PIECES else (1, 0)
            for turn, k in enumerate(blocks):
                nc.tensor.matmul(
                    bank[:],
                    weights[:, k, :],
                    windows[k][:].indirect(offsets[:, first // 16 : (first + width) // 16]),
                    start=(turn == 0),
                    stop=(turn == K_BLOCKS - 1),
                )
            if i % 2 == 0:
                nc.vector.tensor_scalar_add(staged[:, columns], bank[:], bias[:, 0:1])
                nc.sync.dma_start(out[:, columns], staged[:, columns])
            else:
                nc.scalar.activation(
                    staged[:, columns],
                    bank[:],
                    mybir.ActivationFunctionType.Identity,
                    bias=bias[:, 0:1],
                )
                nc.scalar.dma_start(out[:, columns], staged[:, columns])
            first += width
